import numpy as np
import ml_dtypes


def mxq(x, axis, fmt="e4m3"):
    dtype, down = {"e4m3": (ml_dtypes.float8_e4m3fn, 7), "e5m2": (ml_dtypes.float8_e5m2, 14)}[fmt]
    v = np.moveaxis(np.asarray(x, np.float32).astype(ml_dtypes.bfloat16).astype(np.float64), axis, -1)
    blocks = v.reshape(v.shape[:-1] + (-1, 32))
    amax = np.abs(blocks).max(-1, keepdims=True)
    byte = np.maximum(np.where(amax > 0, np.frexp(amax)[1] - 1 + 127, 0) - down, 1)
    scale = np.exp2(byte - 127.0)
    codes = (blocks / scale).astype(np.float32).astype(dtype).astype(np.float64)
    return np.moveaxis((codes * scale).reshape(v.shape), -1, axis)


WIDE = False


def mx_kscale(k):
    if not WIDE:
        return np.ones(k)
    levels = np.array([30, -30])
    if k % 512:
        return np.exp2(np.random.permutation(np.resize(levels, k // 32))).repeat(32)
    a = np.empty((k // 512, 16))
    for p in range(k // 512):
        a[p, :8] = np.random.permutation(np.resize(levels, 8))
        for g in range(8):
            far = levels[np.abs(levels - a[p, g]) >= 10]
            a[p, g + 8] = far[np.random.randint(len(far))]
    return np.exp2(a.ravel()).repeat(32)


def f64(x):
    return np.asarray(x).astype(np.float64)


def striped(idx):
    return np.tile(np.asarray(idx).reshape(-1, 16).T, (8, 1)).astype(np.uint16)


def unstriped(offs):
    return offs[:16].T.reshape(-1).astype(np.int64)


E2M1 = np.array([0.0, 0.5, 1.0, 1.5, 2.0, 3.0, 4.0, 6.0, -0.0, -0.5, -1.0, -1.5, -2.0, -3.0, -4.0, -6.0])


def pack_weight(w, fmt):
    k, n = w.shape
    w = f64(np.asarray(w, np.float32).astype(ml_dtypes.bfloat16)).reshape(k // 32, 32, n)
    amax = np.abs(w).max(1)
    if fmt == "e4m3":
        byte = np.frexp(amax)[1] - 1 + 127 - 7
    else:
        mant, ex = np.frexp(amax / 6.0)
        byte = np.where(mant > 0.5, ex, ex - 1) + 127
    byte = np.clip(np.where(amax > 0, byte, 1), 1, 254)
    scaled = (w * np.exp2(127.0 - byte)[:, None, :]).reshape(k, n).astype(np.float32)
    by_word = np.ascontiguousarray(scaled.reshape(k // 512, 128, 4, n).transpose(0, 1, 3, 2))
    if fmt == "e4m3":
        words = by_word.astype(ml_dtypes.float8_e4m3fn).view(np.uint8)
    else:
        c = by_word.astype(ml_dtypes.float4_e2m1fn).view(np.uint8) & 0xF
        words = (c[..., 0::2] | (c[..., 1::2] << 4)).reshape(k // 512, 128, 2 * n)
    return np.ascontiguousarray(words), np.ascontiguousarray(byte.astype(np.uint8).reshape(k // 512, 16, n))


def unpack_weight(words, scales, fmt):
    g, _, n = scales.shape
    words = np.ascontiguousarray(words).reshape(g, 128, n, -1)
    if fmt == "e4m3":
        vals = words.view(ml_dtypes.float8_e4m3fn).astype(np.float64)
    else:
        nib = np.empty((g, 128, n, 4), np.uint8)
        nib[..., 0::2] = words & 0xF
        nib[..., 1::2] = words >> 4
        vals = E2M1[nib]
    vals = vals * np.repeat(np.exp2(scales.astype(np.float64) - 127.0), 8, axis=1)[..., None]
    return vals.transpose(0, 1, 3, 2).reshape(g * 512, n)


N, K, T, J = 512, 512, 2048, 512


def setup_inputs():
    n = np.random.standard_normal
    idx = np.random.permutation(T)[:J]
    idx2 = np.random.permutation(T)[:J]
    fn = mx_kscale(N)
    wp = pack_weight(n((N, K)) * 1 / np.sqrt(N) * fn[:, None], "e2m1")
    return {
        "g": (n((N, T)) * np.exp(0.5 * n((1, T))) / fn[:, None]).astype(np.float32),
        "rw": (np.random.uniform(0.5, 2.0, (1, J))).astype(np.float32),
        "w_words": wp[0],
        "w_scales": wp[1],
        "run": (0.5 * n((K, J))).astype(np.float32),
        "offs": striped(idx),
        "offs2": striped(idx2),
    }


def reference(g, rw, w_words, w_scales, run, offs, offs2):
    idx = unstriped(offs)
    idx2 = unstriped(offs2)
    wu = unpack_weight(w_words, w_scales, "e2m1")
    d = (f64(g)[:, idx] - f64(g)[:, idx2]) * f64(rw)
    dq = mxq(d, 0, "e5m2")
    p = wu.T @ dq
    y = p + f64(run)
    return y

@@ -1,0 +1,105 @@
+from contextlib import ExitStack
+
+import concourse.mybir as mybir
+from concourse.masks import make_identity
+
+N, K, T, J = 512, 512, 2048, 512
+FLOPS = 2 * N * K * J
+
+F32 = mybir.dt.float32
+BF16 = mybir.dt.bfloat16
+I32 = mybir.dt.int32
+U32 = mybir.dt.uint32
+U16 = mybir.dt.uint16
+U8 = mybir.dt.uint8
+E5M2X4 = mybir.dt.float8_e5m2_x4
+E2M1X4 = mybir.dt.float4_e2m1fn_x4
+ALU = mybir.AluOpType
+
+P = 128
+PACK = 4
+HALF = J // 2
+LIST_COLS = HALF // 16
+
+
+def tile_list_gradient_of_pair_gaps_kernel(tc, g, rw, w_words, w_scales, run, offs, offs2, out):
+    nc = tc.nc
+    with ExitStack() as ctx:
+        keep = ctx.enter_context(tc.tile_pool(name="keep", bufs=1))
+        psum = ctx.enter_context(tc.psum_pool(name="psum", bufs=1))
+
+        first = keep.tile([P, J // 16], U16, name="first")
+        second = keep.tile([P, J // 16], U16, name="second")
+        nc.sync.dma_start(second[:], offs2)
+        nc.sync.dma_start(first[:], offs)
+        rw_cols = keep.tile([P, PACK], F32, name="rw_cols")
+        nc.sync.dma_start(rw_cols[:], rw.rearrange("o (p c) -> (o p) c", c=PACK))
+
+        g_rows = g.rearrange("(p t) c -> t p c", t=PACK)
+        rows = [keep.tile([P, T], F32, name=f"rows{t}") for t in range(PACK)]
+        for t in range(PACK):
+            nc.scalar.dma_start(rows[t][:], g_rows[t])
+
+        w_codes = keep.tile([P, 2 * K], U8, name="w_codes", align_bytes=64)
+        nc.scalar.dma_start(w_codes[:].bitcast(I32), w_words[0].bitcast(I32))
+        run_sb = keep.tile([P, K // P, J], F32, name="run_sb")
+        nc.scalar.dma_start(run_sb[:], run.rearrange("(b p) j -> p b j", p=P))
+        w_exp = keep.tile([P, K], U8, name="w_exp", align_bytes=64)
+        nc.gpsimd.memset(w_exp[:].bitcast(I32), 0)
+        for q in range(4):
+            nc.scalar.dma_start(
+                w_exp[32 * q : 32 * q + 4, :].bitcast(I32),
+                w_scales[0, 4 * q : 4 * q + 4, :].bitcast(I32),
+            )
+
+        ident = keep.tile([P, P], F32, name="ident")
+        make_identity(nc, ident[:])
+        rw_ps = psum.tile([P, PACK, P], F32, name="rw_ps")
+        for c in range(PACK):
+            nc.tensor.transpose(rw_ps[:, c, :], rw_cols[:, c : c + 1].to_broadcast([P, P]), ident[:])
+        rw_all = keep.tile([P, J], F32, name="rw_all")
+        nc.scalar.copy(rw_all[:].rearrange("m (p c) -> m p c", c=PACK), rw_ps[:].rearrange("m c p -> m p c"))
+
+        gaps = [keep.tile([P, PACK, HALF], F32, name=f"gaps{h}") for h in range(2)]
+        for t in range(PACK):
+            picked = [keep.tile([P, HALF], F32, name=f"picked{t}_{h}") for h in range(2)]
+            for h in range(2):
+                cols = slice(h * LIST_COLS, (h + 1) * LIST_COLS)
+                nc.vector.tensor_copy(picked[h][:], rows[t][:].indirect(second[:, cols]))
+            for h in range(2):
+                cols = slice(h * LIST_COLS, (h + 1) * LIST_COLS)
+                nc.vector.tensor_tensor(gaps[h][:, t, :], rows[t][:].indirect(first[:, cols]), picked[h][:], ALU.subtract)
+
+        d_codes = keep.tile([P, J], U32, name="d_codes", align_bytes=64)
+        d_exp = keep.tile([P, J], U8, name="d_exp", align_bytes=64)
+        grouped = [keep.tile([P, HALF, PACK], BF16, name=f"grouped{h}", align_bytes=64) for h in range(2)]
+        for h in range(2):
+            weights = rw_all[:, h * HALF : (h + 1) * HALF].rearrange("p (c i) -> p c i", i=2)
+            nc.vector.tensor_tensor(
+                grouped[h][:].rearrange("p (c i) t -> p c t i", i=2),
+                gaps[h][:].rearrange("p t (c i) -> p c t i", i=2),
+                weights.unsqueeze(2).to_broadcast([P, HALF // 2, PACK, 2]),
+                ALU.mult,
+            )
+        for h in range(2):
+            cols = slice(h * HALF, (h + 1) * HALF)
+            nc.vector.quantize_mx(
+                out=d_codes[:, cols].bitcast(E5M2X4),
+                scales=d_exp[:, cols],
+                in_=grouped[h][:].rearrange("p j t -> p (j t)"),
+            )
+
+        for b in range(K // P):
+            acc = psum.tile([P, J], F32, name=f"acc{b}")
+            nc.tensor.matmul_mx(
+                out=acc[:],
+                lhsT=w_codes[:, 2 * P * b : 2 * P * (b + 1)].bitcast(E2M1X4),
+                lhsT_scale=w_exp[:, P * b : P * (b + 1)],
+                rhs=d_codes[:].bitcast(E5M2X4),
+                rhs_scale=d_exp[:],
+                start=True,
+                stop=True,
+            )
+            result = keep.tile([P, J], F32, name=f"result{b}")
+            nc.vector.tensor_tensor(result[:], acc[:], run_sb[:, b, :], ALU.add)
+            nc.sync.dma_start(out[P * b : P * (b + 1), :], result[:])

@@ -19,6 +19,7 @@ ALU = mybir.AluOpType
 P = 128
 PACK = 4
 HALF = J // 2
+QUARTER = J // 4
 LIST_COLS = HALF // 16
 
 
@@ -32,14 +33,14 @@ def tile_list_gradient_of_pair_gaps_kernel(tc, g, rw, w_words, w_scales, run, of
         second = keep.tile([P, J // 16], U16, name="second")
         nc.sync.dma_start(second[:], offs2)
         nc.sync.dma_start(first[:], offs)
-        rw_cols = keep.tile([P, PACK], F32, name="rw_cols")
-        nc.sync.dma_start(rw_cols[:], rw.rearrange("o (p c) -> (o p) c", c=PACK))
 
         g_rows = g.rearrange("(p t) c -> t p c", t=PACK)
         rows = [keep.tile([P, T], F32, name=f"rows{t}") for t in range(PACK)]
         for t in range(PACK):
             nc.scalar.dma_start(rows[t][:], g_rows[t])
 
+        rw_cols = keep.tile([P, PACK], F32, name="rw_cols")
+        nc.scalar.dma_start(rw_cols[:], rw.rearrange("o (p c) -> (o p) c", c=PACK))
         w_codes = keep.tile([P, 2 * K], U8, name="w_codes", align_bytes=64)
         nc.scalar.dma_start(w_codes[:].bitcast(I32), w_words[0].bitcast(I32))
         run_sb = keep.tile([P, K // P, J], F32, name="run_sb")
@@ -54,11 +55,15 @@ def tile_list_gradient_of_pair_gaps_kernel(tc, g, rw, w_words, w_scales, run, of
 
         ident = keep.tile([P, P], F32, name="ident")
         make_identity(nc, ident[:])
-        rw_ps = psum.tile([P, PACK, P], F32, name="rw_ps")
+        rw_ps = psum.tile([P, J], F32, name="rw_ps")
         for c in range(PACK):
-            nc.tensor.transpose(rw_ps[:, c, :], rw_cols[:, c : c + 1].to_broadcast([P, P]), ident[:])
-        rw_all = keep.tile([P, J], F32, name="rw_all")
-        nc.scalar.copy(rw_all[:].rearrange("m (p c) -> m p c", c=PACK), rw_ps[:].rearrange("m c p -> m p c"))
+            nc.tensor.transpose(
+                rw_ps[:].rearrange("m (p c) -> m c p", c=PACK)[:, c, :],
+                rw_cols[:, c : c + 1].to_broadcast([P, P]),
+                ident[:],
+            )
+        rw_last = keep.tile([P, QUARTER], F32, name="rw_last")
+        nc.scalar.copy(rw_last[:], rw_ps[:, J - QUARTER :])
 
         gaps = [keep.tile([P, PACK, HALF], F32, name=f"gaps{h}") for h in range(2)]
         for t in range(PACK):
@@ -72,21 +77,29 @@ def tile_list_gradient_of_pair_gaps_kernel(tc, g, rw, w_words, w_scales, run, of
 
         d_codes = keep.tile([P, J], U32, name="d_codes", align_bytes=64)
         d_exp = keep.tile([P, J], U8, name="d_exp", align_bytes=64)
-        grouped = [keep.tile([P, HALF, PACK], BF16, name=f"grouped{h}", align_bytes=64) for h in range(2)]
-        for h in range(2):
-            weights = rw_all[:, h * HALF : (h + 1) * HALF].rearrange("p (c i) -> p c i", i=2)
+        shares = [(0, HALF), (HALF, QUARTER), (HALF + QUARTER, QUARTER)]
+        grouped = [keep.tile([P, n, PACK], BF16, name=f"grouped{j0}", align_bytes=64) for j0, n in shares]
+        nc.gpsimd.tensor_tensor(
+            grouped[2][:],
+            gaps[1][:, :, QUARTER:].rearrange("p t j -> p j t"),
+            rw_last[:].unsqueeze(2).to_broadcast([P, QUARTER, PACK]),
+            ALU.mult,
+        )
+        for s in range(2):
+            j0, n = shares[s]
+            weights = rw_ps[:, j0 : j0 + n].rearrange("p (c i) -> p c i", i=2)
             nc.vector.tensor_tensor(
-                grouped[h][:].rearrange("p (c i) t -> p c t i", i=2),
-                gaps[h][:].rearrange("p t (c i) -> p c t i", i=2),
-                weights.unsqueeze(2).to_broadcast([P, HALF // 2, PACK, 2]),
+                grouped[s][:].rearrange("p (c i) t -> p c t i", i=2),
+                gaps[s][:, :, :n].rearrange("p t (c i) -> p c t i", i=2),
+                weights.unsqueeze(2).to_broadcast([P, n // 2, PACK, 2]),
                 ALU.mult,
             )
-        for h in range(2):
-            cols = slice(h * HALF, (h + 1) * HALF)
+        for s in range(3):
+            j0, n = shares[s]
             nc.vector.quantize_mx(
-                out=d_codes[:, cols].bitcast(E5M2X4),
-                scales=d_exp[:, cols],
-                in_=grouped[h][:].rearrange("p j t -> p (j t)"),
+                out=d_codes[:, j0 : j0 + n].bitcast(E5M2X4),
+                scales=d_exp[:, j0 : j0 + n],
+                in_=grouped[s][:].rearrange("p j t -> p (j t)"),
             )
 
         for b in range(K // P):
@@ -100,6 +113,9 @@ def tile_list_gradient_of_pair_gaps_kernel(tc, g, rw, w_words, w_scales, run, of
                 start=True,
                 stop=True,
             )
-            result = keep.tile([P, J], F32, name=f"result{b}")
-            nc.vector.tensor_tensor(result[:], acc[:], run_sb[:, b, :], ALU.add)
-            nc.sync.dma_start(out[P * b : P * (b + 1), :], result[:])
+            pieces = 2 if b in (0, K // P - 1) else 1
+            for u in range(pieces):
+                cols = slice(u * J // pieces, (u + 1) * J // pieces)
+                result = keep.tile([P, J // pieces], F32, name=f"result{b}_{u}")
+                nc.vector.tensor_tensor(result[:], acc[:, cols], run_sb[:, b, cols], ALU.add)
+                nc.sync.dma_start(out[P * b : P * (b + 1), cols], result[:])

@@ -20,7 +20,6 @@ P = 128
 PACK = 4
 HALF = J // 2
 QUARTER = J // 4
-LIST_COLS = HALF // 16
 
 
 def tile_list_gradient_of_pair_gaps_kernel(tc, g, rw, w_words, w_scales, run, offs, offs2, out):
@@ -29,26 +28,25 @@ def tile_list_gradient_of_pair_gaps_kernel(tc, g, rw, w_words, w_scales, run, of
         keep = ctx.enter_context(tc.tile_pool(name="keep", bufs=1))
         psum = ctx.enter_context(tc.psum_pool(name="psum", bufs=1))
 
-        first = keep.tile([P, J // 16], U16, name="first")
-        second = keep.tile([P, J // 16], U16, name="second")
-        nc.sync.dma_start(second[:], offs2)
-        nc.sync.dma_start(first[:], offs)
-
         g_rows = g.rearrange("(p t) c -> t p c", t=PACK)
         rows = [keep.tile([P, T], F32, name=f"rows{t}") for t in range(PACK)]
-        for t in range(PACK):
-            nc.scalar.dma_start(rows[t][:], g_rows[t])
-
+        first = keep.tile([P, J // 16], U16, name="first")
+        second = keep.tile([P, J // 16], U16, name="second")
+        nc.sync.dma_start(rows[0][:], g_rows[0])
+        nc.sync.dma_start(second[:], offs2)
+        nc.sync.dma_start(first[:], offs)
+        for t in range(1, PACK):
+            nc.sync.dma_start(rows[t][:], g_rows[t])
         rw_cols = keep.tile([P, PACK], F32, name="rw_cols")
         nc.scalar.dma_start(rw_cols[:], rw.rearrange("o (p c) -> (o p) c", c=PACK))
         w_codes = keep.tile([P, 2 * K], U8, name="w_codes", align_bytes=64)
-        nc.scalar.dma_start(w_codes[:].bitcast(I32), w_words[0].bitcast(I32))
+        nc.sync.dma_start(w_codes[:].bitcast(I32), w_words[0].bitcast(I32))
         run_sb = keep.tile([P, K // P, J], F32, name="run_sb")
-        nc.scalar.dma_start(run_sb[:], run.rearrange("(b p) j -> p b j", p=P))
+        nc.sync.dma_start(run_sb[:], run.rearrange("(b p) j -> p b j", p=P))
         w_exp = keep.tile([P, K], U8, name="w_exp", align_bytes=64)
         nc.gpsimd.memset(w_exp[:].bitcast(I32), 0)
         for q in range(4):
-            nc.scalar.dma_start(
+            nc.sync.dma_start(
                 w_exp[32 * q : 32 * q + 4, :].bitcast(I32),
                 w_scales[0, 4 * q : 4 * q + 4, :].bitcast(I32),
             )
@@ -62,39 +60,38 @@ def tile_list_gradient_of_pair_gaps_kernel(tc, g, rw, w_words, w_scales, run, of
                 rw_cols[:, c : c + 1].to_broadcast([P, P]),
                 ident[:],
             )
-        rw_last = keep.tile([P, QUARTER], F32, name="rw_last")
-        nc.scalar.copy(rw_last[:], rw_ps[:, J - QUARTER :])
+        rw_upper = keep.tile([P, HALF], F32, name="rw_upper")
+        nc.scalar.copy(rw_upper[:], rw_ps[:, HALF:])
 
-        gaps = [keep.tile([P, PACK, HALF], F32, name=f"gaps{h}") for h in range(2)]
+        shares = [(0, QUARTER), (HALF, HALF), (QUARTER, QUARTER)]
+        gaps = [keep.tile([P, PACK, n], F32, name=f"gaps{j0}") for j0, n in shares]
+        grouped = [keep.tile([P, n, PACK], BF16, name=f"grouped{j0}", align_bytes=64) for j0, n in shares]
         for t in range(PACK):
             picked = [keep.tile([P, HALF], F32, name=f"picked{t}_{h}") for h in range(2)]
             for h in range(2):
-                cols = slice(h * LIST_COLS, (h + 1) * LIST_COLS)
+                cols = slice(h * HALF // 16, (h + 1) * HALF // 16)
                 nc.vector.tensor_copy(picked[h][:], rows[t][:].indirect(second[:, cols]))
-            for h in range(2):
-                cols = slice(h * LIST_COLS, (h + 1) * LIST_COLS)
-                nc.vector.tensor_tensor(gaps[h][:, t, :], rows[t][:].indirect(first[:, cols]), picked[h][:], ALU.subtract)
+            for s, (j0, n) in enumerate(shares):
+                nc.vector.tensor_tensor(
+                    gaps[s][:, t, :],
+                    rows[t][:].indirect(first[:, j0 // 16 : (j0 + n) // 16]),
+                    picked[j0 // HALF][:, j0 % HALF : j0 % HALF + n],
+                    ALU.subtract,
+                )
+            nc.gpsimd.tensor_tensor(grouped[1][:, :, t], gaps[1][:, t, :], rw_upper[:], ALU.mult)
 
         d_codes = keep.tile([P, J], U32, name="d_codes", align_bytes=64)
         d_exp = keep.tile([P, J], U8, name="d_exp", align_bytes=64)
-        shares = [(0, HALF), (HALF, QUARTER), (HALF + QUARTER, QUARTER)]
-        grouped = [keep.tile([P, n, PACK], BF16, name=f"grouped{j0}", align_bytes=64) for j0, n in shares]
-        nc.gpsimd.tensor_tensor(
-            grouped[2][:],
-            gaps[1][:, :, QUARTER:].rearrange("p t j -> p j t"),
-            rw_last[:].unsqueeze(2).to_broadcast([P, QUARTER, PACK]),
-            ALU.mult,
-        )
-        for s in range(2):
+        for s in (0, 2):
             j0, n = shares[s]
             weights = rw_ps[:, j0 : j0 + n].rearrange("p (c i) -> p c i", i=2)
             nc.vector.tensor_tensor(
                 grouped[s][:].rearrange("p (c i) t -> p c t i", i=2),
-                gaps[s][:, :, :n].rearrange("p t (c i) -> p c t i", i=2),
+                gaps[s][:].rearrange("p t (c i) -> p c t i", i=2),
                 weights.unsqueeze(2).to_broadcast([P, n // 2, PACK, 2]),
                 ALU.mult,
             )
-        for s in range(3):
+        for s in (0, 2, 1):
             j0, n = shares[s]
             nc.vector.quantize_mx(
                 out=d_codes[:, j0 : j0 + n].bitcast(E5M2X4),

from contextlib import ExitStack

import concourse.mybir as mybir
from concourse.masks import make_identity

N, K, T, J = 512, 512, 2048, 512
FLOPS = 2 * N * K * J

F32 = mybir.dt.float32
BF16 = mybir.dt.bfloat16
I32 = mybir.dt.int32
U32 = mybir.dt.uint32
U16 = mybir.dt.uint16
U8 = mybir.dt.uint8
E5M2X4 = mybir.dt.float8_e5m2_x4
E2M1X4 = mybir.dt.float4_e2m1fn_x4
ALU = mybir.AluOpType

P = 128
PACK = 4
HALF = J // 2
QUARTER = J // 4


def tile_list_gradient_of_pair_gaps_kernel(tc, g, rw, w_words, w_scales, run, offs, offs2, out):
    nc = tc.nc
    with ExitStack() as ctx:
        keep = ctx.enter_context(tc.tile_pool(name="keep", bufs=1))
        psum = ctx.enter_context(tc.psum_pool(name="psum", bufs=1))

        g_rows = g.rearrange("(p t) c -> t p c", t=PACK)
        rows = [keep.tile([P, T], F32, name=f"rows{t}") for t in range(PACK)]
        first = keep.tile([P, J // 16], U16, name="first")
        second = keep.tile([P, J // 16], U16, name="second")
        nc.sync.dma_start(rows[0][:], g_rows[0])
        nc.sync.dma_start(second[:], offs2)
        nc.sync.dma_start(first[:], offs)
        for t in range(1, PACK):
            nc.sync.dma_start(rows[t][:], g_rows[t])
        rw_cols = keep.tile([P, PACK], F32, name="rw_cols")
        nc.scalar.dma_start(rw_cols[:], rw.rearrange("o (p c) -> (o p) c", c=PACK))
        w_codes = keep.tile([P, 2 * K], U8, name="w_codes", align_bytes=64)
        nc.sync.dma_start(w_codes[:].bitcast(I32), w_words[0].bitcast(I32))
        run_sb = keep.tile([P, K // P, J], F32, name="run_sb")
        nc.sync.dma_start(run_sb[:], run.rearrange("(b p) j -> p b j", p=P))
        w_exp = keep.tile([P, K], U8, name="w_exp", align_bytes=64)
        nc.gpsimd.memset(w_exp[:].bitcast(I32), 0)
        for q in range(4):
            nc.sync.dma_start(
                w_exp[32 * q : 32 * q + 4, :].bitcast(I32),
                w_scales[0, 4 * q : 4 * q + 4, :].bitcast(I32),
            )

        ident = keep.tile([P, P], F32, name="ident")
        make_identity(nc, ident[:])
        rw_ps = psum.tile([P, J], F32, name="rw_ps")
        for c in range(PACK):
            nc.tensor.transpose(
                rw_ps[:].rearrange("m (p c) -> m c p", c=PACK)[:, c, :],
                rw_cols[:, c : c + 1].to_broadcast([P, P]),
                ident[:],
            )
        rw_upper = keep.tile([P, HALF], F32, name="rw_upper")
        nc.scalar.copy(rw_upper[:], rw_ps[:, HALF:])

        shares = [(0, QUARTER), (HALF, HALF), (QUARTER, QUARTER)]
        gaps = [keep.tile([P, PACK, n], F32, name=f"gaps{j0}") for j0, n in shares]
        grouped = [keep.tile([P, n, PACK], BF16, name=f"grouped{j0}", align_bytes=64) for j0, n in shares]
        for t in range(PACK):
            picked = [keep.tile([P, HALF], F32, name=f"picked{t}_{h}") for h in range(2)]
            for h in range(2):
                cols = slice(h * HALF // 16, (h + 1) * HALF // 16)
                nc.vector.tensor_copy(picked[h][:], rows[t][:].indirect(second[:, cols]))
            for s, (j0, n) in enumerate(shares):
                nc.vector.tensor_tensor(
                    gaps[s][:, t, :],
                    rows[t][:].indirect(first[:, j0 // 16 : (j0 + n) // 16]),
                    picked[j0 // HALF][:, j0 % HALF : j0 % HALF + n],
                    ALU.subtract,
                )
            nc.gpsimd.tensor_tensor(grouped[1][:, :, t], gaps[1][:, t, :], rw_upper[:], ALU.mult)

        d_codes = keep.tile([P, J], U32, name="d_codes", align_bytes=64)
        d_exp = keep.tile([P, J], U8, name="d_exp", align_bytes=64)
        for s in (0, 2):
            j0, n = shares[s]
            weights = rw_ps[:, j0 : j0 + n].rearrange("p (c i) -> p c i", i=2)
            nc.vector.tensor_tensor(
                grouped[s][:].rearrange("p (c i) t -> p c t i", i=2),
                gaps[s][:].rearrange("p t (c i) -> p c t i", i=2),
                weights.unsqueeze(2).to_broadcast([P, n // 2, PACK, 2]),
                ALU.mult,
            )
        for s in (0, 2, 1):
            j0, n = shares[s]
            nc.vector.quantize_mx(
                out=d_codes[:, j0 : j0 + n].bitcast(E5M2X4),
                scales=d_exp[:, j0 : j0 + n],
                in_=grouped[s][:].rearrange("p j t -> p (j t)"),
            )

        for b in range(K // P):
            acc = psum.tile([P, J], F32, name=f"acc{b}")
            nc.tensor.matmul_mx(
                out=acc[:],
                lhsT=w_codes[:, 2 * P * b : 2 * P * (b + 1)].bitcast(E2M1X4),
                lhsT_scale=w_exp[:, P * b : P * (b + 1)],
                rhs=d_codes[:].bitcast(E5M2X4),
                rhs_scale=d_exp[:],
                start=True,
                stop=True,
            )
            pieces = 2 if b in (0, K // P - 1) else 1
            for u in range(pieces):
                cols = slice(u * J // pieces, (u + 1) * J // pieces)
                result = keep.tile([P, J // pieces], F32, name=f"result{b}_{u}")
                nc.vector.tensor_tensor(result[:], acc[:, cols], run_sb[:, b, cols], ALU.add)
                nc.sync.dma_start(out[P * b : P * (b + 1), cols], result[:])
